import numpy as np, ml_dtypes
CORES = [8,136,40,168]
N = 4
NB, TK, FT = 4, 32, 4
def setup_inputs(rng):
    return {"x": rng.standard_normal((N, NB, 128, TK), dtype=np.float32).astype(ml_dtypes.bfloat16), "w1": (rng.standard_normal((N, 128, FT * 128), dtype=np.float32) / 8).astype(ml_dtypes.bfloat16), "w2": (rng.standard_normal((N, 128, FT * 128), dtype=np.float32) / np.float32(8 * np.sqrt(FT))).astype(ml_dtypes.bfloat16)}
def setup_inputs_big(rng):
    d = setup_inputs(rng)
    for k in ("x",): d[k] = (d[k].astype(np.float32) * 1048576.0).astype(d[k].dtype)
    return d
def setup_inputs_small(rng):
    d = setup_inputs(rng)
    for k in ("x",): d[k] = (d[k].astype(np.float32) * (1 / 1048576.0)).astype(d[k].dtype)
    return d
def reference(x, w1, w2):
    W1, W2 = w1.astype(np.float64), w2.astype(np.float64)
    a = x[0].astype(np.float64)
    for s in range(N):
        a = sum(np.einsum("kf,bkn->bfn", W2[s][:, 128 * f:128 * f + 128], np.maximum(np.einsum("kf,bkn->bfn", W1[s][:, 128 * f:128 * f + 128], a), 0.0)) for f in range(FT))
    y = np.full(x.shape, np.nan, ml_dtypes.bfloat16)
    y[N - 1] = a.astype(ml_dtypes.bfloat16)
    return {"y": y}

@@ -1,0 +1,129 @@
+from concourse.mybir import AluOpType
+
+N, NB, TK, FT = 4, 4, 32, 4
+P = 128
+COLS = NB * TK
+WC = FT * P
+SITE = [0, 1, 3, 3]
+EW = 8
+EA = 8
+
+
+def _slot(s):
+    return [t for t in range(N) if SITE[t] == SITE[s]].index(s)
+
+
+def _own(r):
+    return _slot(r) if SITE[r] == r else SITE.count(r)
+
+
+NSLOT = max(SITE.count(r) + (0 if SITE[r] == r else 1) for r in range(N))
+
+SCRATCH = {"zero": ("sbuf", [P, COLS], "float32"), "po": ("psum", [P, 512], "float32")}
+for _k in range(NSLOT):
+    SCRATCH["wt%d" % _k] = ("sbuf", [P, 2 * WC], "bfloat16")
+    SCRATCH["h%d" % _k] = ("sbuf", [P, FT * COLS], "bfloat16")
+for _s in range(N + 1):
+    SCRATCH["a%d" % _s] = ("sbuf", [P, COLS], "bfloat16")
+for _f in range(FT):
+    SCRATCH["ph%d" % _f] = ("psum", [P, 512], "float32")
+
+SEMAPHORES = ["z", "snt", "lw0", "lw1"]
+SEMAPHORES += ["lx%d" % m for m in range(NB)] + ["st%d" % m for m in range(NB)]
+SEMAPHORES += ["ww%d_%d" % (s, i) for s in range(N) for i in range(2)]
+SEMAPHORES += ["aa%d" % s for s in range(N + 1)]
+SEMAPHORES += ["m1_%d_%d" % (s, f) for s in range(N) for f in range(FT)]
+SEMAPHORES += ["r_%d_%d" % (s, f) for s in range(N) for f in range(FT)]
+SEMAPHORES += ["m2_%d" % s for s in range(N)] + ["c_%d" % s for s in range(N)]
+
+
+def _engines(mask, n):
+    bits = [b for b in range(16) if (mask >> b) & 1]
+    step = max(1, len(bits) // n)
+    out = 0
+    for b in bits[::step][:n]:
+        out |= 1 << b
+    return out
+
+
+def rank_program(g, core, T, topo):
+    r = T.rank_of(core)
+    if r is None:
+        return
+    sem = T.sem
+    te, ve = g.tensor, g.vector
+    mine = [s for s in range(N) if SITE[s] == r]
+    sent = 0
+
+    wown = T["wt%d" % _own(r)]
+    g.sync.dma_start(wown[:, 0:WC], T.w1[:, :]).then_inc(sem.lw0, 16)
+    if r == 0:
+        for m in range(NB):
+            q = g.sync if m < NB // 2 else g.scalar
+            q.dma_start(T.a0[:, m * TK:(m + 1) * TK], T.x[m]).then_inc(sem["lx%d" % m], 16)
+    g.scalar.dma_start(wown[:, WC:2 * WC], T.w2[:, :]).then_inc(sem.lw1, 16)
+
+    if SITE[r] != r:
+        dst = T.cores[SITE[r]]
+        rid, pid = topo.addr(dst, core)
+        mk = _engines(topo.mask(core, dst), EW)
+        for i in range(2):
+            g.wait_ge(sem["lw%d" % i], 16)
+            g.remote_dma(out_ap=T["wt%d" % _slot(r)][:, i * WC:(i + 1) * WC], in_ap=wown[:, i * WC:(i + 1) * WC],
+                         remote_sem=sem["ww%d_%d" % (r, i)], local_sem=sem.snt,
+                         pid=pid, routing_id=rid, dma_engine_mask=mk)
+            sent += EW
+
+    if mine:
+        ve.memset(T.zero[:], 0.0).then_inc(sem.z, 1)
+        ve.wait_ge(sem.z, 1)
+
+    for s in mine:
+        a_in, a_out = T["a%d" % s], T["a%d" % (s + 1)]
+        w, h = T["wt%d" % _slot(s)], T["h%d" % _slot(s)]
+        if s == 0:
+            for m in range(NB):
+                te.wait_ge(sem["lx%d" % m], 16)
+        elif SITE[s - 1] == r:
+            te.wait_ge(sem["c_%d" % (s - 1)], 1)
+        else:
+            te.wait_ge(sem["aa%d" % s], EA)
+        for i in range(2):
+            if s == r:
+                te.wait_ge(sem["lw%d" % i], 16)
+            else:
+                te.wait_ge(sem["ww%d_%d" % (s, i)], EW)
+            for f in range(FT):
+                if i == 0:
+                    te.matmul(out=T["ph%d" % f][:, 0:COLS], lhsT=w[:, f * P:(f + 1) * P], rhs=a_in[:],
+                              start=True, stop=True).then_inc(sem["m1_%d_%d" % (s, f)], 1)
+                else:
+                    te.wait_ge(sem["r_%d_%d" % (s, f)], 1)
+                    te.matmul(out=T.po[:, 0:COLS], lhsT=w[:, WC + f * P:WC + (f + 1) * P],
+                              rhs=h[:, f * COLS:(f + 1) * COLS],
+                              start=(f == 0), stop=(f == FT - 1)).then_inc(sem["m2_%d" % s], 1)
+        for f in range(FT):
+            ve.wait_ge(sem["m1_%d_%d" % (s, f)], 1)
+            ve.tensor_tensor(out=h[:, f * COLS:(f + 1) * COLS], in0=T["ph%d" % f][:, 0:COLS], in1=T.zero[:],
+                             op=AluOpType.max).then_inc(sem["r_%d_%d" % (s, f)], 1)
+        ve.wait_ge(sem["m2_%d" % s], FT)
+        ve.tensor_copy(out=a_out[:], in_=T.po[:, 0:COLS]).then_inc(sem["c_%d" % s], 1)
+
+        if s == N - 1:
+            g.sync.wait_ge(sem["c_%d" % s], 1)
+            g.scalar.wait_ge(sem["c_%d" % s], 1)
+            for m in range(NB):
+                q = g.sync if m % 2 == 0 else g.scalar
+                q.dma_start(T.y[m], a_out[:, m * TK:(m + 1) * TK]).then_inc(sem["st%d" % m], 16)
+            for m in range(NB):
+                g.wait_ge(sem["st%d" % m], 16)
+        elif SITE[s + 1] != r:
+            dst = T.cores[SITE[s + 1]]
+            rid, pid = topo.addr(dst, core)
+            g.wait_ge(sem["c_%d" % s], 1)
+            g.remote_dma(out_ap=a_out[:], in_ap=a_out[:], remote_sem=sem["aa%d" % (s + 1)], local_sem=sem.snt,
+                         pid=pid, routing_id=rid, dma_engine_mask=_engines(topo.mask(core, dst), EA))
+            sent += EA
+
+    if sent:
+        g.wait_ge(sem.snt, sent)

@@ -4,37 +4,32 @@ N, NB, TK, FT = 4, 4, 32, 4
 P = 128
 COLS = NB * TK
 WC = FT * P
-SITE = [0, 1, 3, 3]
+OFF = FT - 1
+KEEP = OFF * P
 EW = 8
 EA = 8
 
-
-def _slot(s):
-    return [t for t in range(N) if SITE[t] == SITE[s]].index(s)
-
-
-def _own(r):
-    return _slot(r) if SITE[r] == r else SITE.count(r)
-
-
-NSLOT = max(SITE.count(r) + (0 if SITE[r] == r else 1) for r in range(N))
-
-SCRATCH = {"zero": ("sbuf", [P, COLS], "float32"), "po": ("psum", [P, 512], "float32")}
-for _k in range(NSLOT):
-    SCRATCH["wt%d" % _k] = ("sbuf", [P, 2 * WC], "bfloat16")
+SCRATCH = {
+    "zero": ("sbuf", [P, COLS], "float32"),
+    "po": ("psum", [P, 512], "float32"),
+    "wt0": ("sbuf", [P, 2 * WC], "bfloat16"),
+    "wt1": ("sbuf", [P, 2 * WC], "bfloat16"),
+    "tw": ("sbuf", [P, 2 * P], "bfloat16"),
+    "pb": ("sbuf", [P, COLS], "bfloat16"),
+}
+for _k in range(3):
     SCRATCH["h%d" % _k] = ("sbuf", [P, FT * COLS], "bfloat16")
 for _s in range(N + 1):
     SCRATCH["a%d" % _s] = ("sbuf", [P, COLS], "bfloat16")
 for _f in range(FT):
     SCRATCH["ph%d" % _f] = ("psum", [P, 512], "float32")
 
-SEMAPHORES = ["z", "snt", "lw0", "lw1"]
+TAGS = ["s0", "s1", "s2", "s3", "t"]
+SEMAPHORES = ["z", "snt", "lw0", "lw1", "lt0", "lt1", "ww0", "ww1", "tarr", "aa1", "aa2", "pbarr"]
 SEMAPHORES += ["lx%d" % m for m in range(NB)] + ["st%d" % m for m in range(NB)]
-SEMAPHORES += ["ww%d_%d" % (s, i) for s in range(N) for i in range(2)]
-SEMAPHORES += ["aa%d" % s for s in range(N + 1)]
-SEMAPHORES += ["m1_%d_%d" % (s, f) for s in range(N) for f in range(FT)]
-SEMAPHORES += ["r_%d_%d" % (s, f) for s in range(N) for f in range(FT)]
-SEMAPHORES += ["m2_%d" % s for s in range(N)] + ["c_%d" % s for s in range(N)]
+SEMAPHORES += ["m1_%s_%d" % (t, f) for t in TAGS for f in range(FT)]
+SEMAPHORES += ["r_%s_%d" % (t, f) for t in TAGS for f in range(FT)]
+SEMAPHORES += ["m2_%s" % t for t in TAGS] + ["c_%s" % t for t in TAGS]
 
 
 def _engines(mask, n):
@@ -46,84 +41,101 @@ def _engines(mask, n):
     return out
 
 
+def _map(g, T, tag, tiles, w1, w2, parts, w2waits, h, out):
+    te, ve, sem = g.tensor, g.vector, T.sem
+    for pi, (rhs, waits) in enumerate(parts):
+        for name, val in waits:
+            te.wait_ge(sem[name], val)
+        for f in tiles:
+            te.matmul(out=T["ph%d" % f][:, 0:COLS], lhsT=w1(f), rhs=rhs[:],
+                      start=(pi == 0), stop=(pi == len(parts) - 1)).then_inc(sem["m1_%s_%d" % (tag, f)], 1)
+    for name, val in w2waits:
+        te.wait_ge(sem[name], val)
+    for j, f in enumerate(tiles):
+        te.wait_ge(sem["r_%s_%d" % (tag, f)], 1)
+        te.matmul(out=T.po[:, 0:COLS], lhsT=w2(f), rhs=h[:, f * COLS:(f + 1) * COLS],
+                  start=(j == 0), stop=(j == len(tiles) - 1)).then_inc(sem["m2_%s" % tag], 1)
+    for f in tiles:
+        ve.wait_ge(sem["m1_%s_%d" % (tag, f)], len(parts))
+        ve.tensor_tensor(out=h[:, f * COLS:(f + 1) * COLS], in0=T["ph%d" % f][:, 0:COLS], in1=T.zero[:],
+                         op=AluOpType.max).then_inc(sem["r_%s_%d" % (tag, f)], 1)
+    ve.wait_ge(sem["m2_%s" % tag], len(tiles))
+    ve.tensor_copy(out=out[:], in_=T.po[:, 0:COLS]).then_inc(sem["c_%s" % tag], 1)
+
+
 def rank_program(g, core, T, topo):
     r = T.rank_of(core)
     if r is None:
         return
     sem = T.sem
-    te, ve = g.tensor, g.vector
-    mine = [s for s in range(N) if SITE[s] == r]
-    sent = 0
+    last = N - 1
+    sent = [0]
 
-    wown = T["wt%d" % _own(r)]
-    g.sync.dma_start(wown[:, 0:WC], T.w1[:, :]).then_inc(sem.lw0, 16)
+    def write(dst_rank, dst_ap, src_ap, arrive, n):
+        dst = T.cores[dst_rank]
+        rid, pid = topo.addr(dst, core)
+        g.remote_dma(out_ap=dst_ap, in_ap=src_ap, remote_sem=sem[arrive], local_sem=sem.snt,
+                     pid=pid, routing_id=rid, dma_engine_mask=_engines(topo.mask(core, dst), n))
+        sent[0] += n
+
+    def tiles_of(w):
+        return (lambda f: w[:, f * P:(f + 1) * P]), (lambda f: w[:, WC + f * P:WC + (f + 1) * P])
+
+    if r != 2:
+        g.vector.memset(T.zero[:], 0.0).then_inc(sem.z, 1)
+        g.vector.wait_ge(sem.z, 1)
+
     if r == 0:
+        g.sync.dma_start(T.wt0[:, 0:WC], T.w1[:, :]).then_inc(sem.lw0, 16)
         for m in range(NB):
             q = g.sync if m < NB // 2 else g.scalar
             q.dma_start(T.a0[:, m * TK:(m + 1) * TK], T.x[m]).then_inc(sem["lx%d" % m], 16)
-    g.scalar.dma_start(wown[:, WC:2 * WC], T.w2[:, :]).then_inc(sem.lw1, 16)
+        g.scalar.dma_start(T.wt0[:, WC:2 * WC], T.w2[:, :]).then_inc(sem.lw1, 16)
+        w1, w2 = tiles_of(T.wt0)
+        _map(g, T, "s0", range(FT), w1, w2, [(T.a0, [("lx%d" % m, 16) for m in range(NB)] + [("lw0", 16)])],
+             [("lw1", 16)], T.h0, T.a1)
+        g.wait_ge(sem.c_s0, 1)
+        write(1, T.a1[:], T.a1[:], "aa1", EA)
+        _map(g, T, "t", [OFF], lambda f: T.tw[:, 0:P], lambda f: T.tw[:, P:2 * P],
+             [(T.a1, [("c_s0", 1), ("tarr", EW)])], [], T.h2, T.pb)
+        g.wait_ge(sem.c_t, 1)
+        write(last, T.pb[:], T.pb[:], "pbarr", EA)
 
-    if SITE[r] != r:
-        dst = T.cores[SITE[r]]
-        rid, pid = topo.addr(dst, core)
-        mk = _engines(topo.mask(core, dst), EW)
+    if r == 1:
+        g.sync.dma_start(T.tw[:, 0:P], T.w1[:, KEEP:WC]).then_inc(sem.lt0, 16)
+        g.scalar.dma_start(T.tw[:, P:2 * P], T.w2[:, KEEP:WC]).then_inc(sem.lt1, 16)
+        g.sync.dma_start(T.wt0[:, 0:KEEP], T.w1[:, 0:KEEP]).then_inc(sem.lw0, 16)
+        g.scalar.dma_start(T.wt0[:, WC:WC + KEEP], T.w2[:, 0:KEEP]).then_inc(sem.lw1, 16)
+        g.wait_ge(sem.lt0, 16)
+        g.wait_ge(sem.lt1, 16)
+        write(0, T.tw[:], T.tw[:], "tarr", EW)
+        w1, w2 = tiles_of(T.wt0)
+        _map(g, T, "s1", range(OFF), w1, w2, [(T.a1, [("aa1", EA), ("lw0", 16)])], [("lw1", 16)], T.h0, T.a2)
+        g.wait_ge(sem.c_s1, 1)
+        write(last, T.a2[:], T.a2[:], "aa2", EA)
+
+    if r == 2:
+        g.sync.dma_start(T.wt0[:, 0:WC], T.w1[:, :]).then_inc(sem.lw0, 16)
+        g.scalar.dma_start(T.wt0[:, WC:2 * WC], T.w2[:, :]).then_inc(sem.lw1, 16)
         for i in range(2):
             g.wait_ge(sem["lw%d" % i], 16)
-            g.remote_dma(out_ap=T["wt%d" % _slot(r)][:, i * WC:(i + 1) * WC], in_ap=wown[:, i * WC:(i + 1) * WC],
-                         remote_sem=sem["ww%d_%d" % (r, i)], local_sem=sem.snt,
-                         pid=pid, routing_id=rid, dma_engine_mask=mk)
-            sent += EW
+            write(last, T.wt0[:, i * WC:(i + 1) * WC], T.wt0[:, i * WC:(i + 1) * WC], "ww%d" % i, EW)
 
-    if mine:
-        ve.memset(T.zero[:], 0.0).then_inc(sem.z, 1)
-        ve.wait_ge(sem.z, 1)
+    if r == last:
+        g.sync.dma_start(T.wt1[:, 0:WC], T.w1[:, :]).then_inc(sem.lw0, 16)
+        g.scalar.dma_start(T.wt1[:, WC:2 * WC], T.w2[:, :]).then_inc(sem.lw1, 16)
+        w1, w2 = tiles_of(T.wt0)
+        _map(g, T, "s2", range(FT), w1, w2, [(T.pb, [("pbarr", EA), ("ww0", EW)]), (T.a2, [("aa2", EA)])],
+             [("ww1", EW)], T.h0, T.a3)
+        w1, w2 = tiles_of(T.wt1)
+        _map(g, T, "s3", range(FT), w1, w2, [(T.a3, [("c_s2", 1), ("lw0", 16)])], [("lw1", 16)], T.h1, T.a4)
+        g.sync.wait_ge(sem.c_s3, 1)
+        g.scalar.wait_ge(sem.c_s3, 1)
+        for m in range(NB):
+            q = g.sync if m % 2 == 0 else g.scalar
+            q.dma_start(T.y[m], T.a4[:, m * TK:(m + 1) * TK]).then_inc(sem["st%d" % m], 16)
+        for m in range(NB):
+            g.wait_ge(sem["st%d" % m], 16)
 
-    for s in mine:
-        a_in, a_out = T["a%d" % s], T["a%d" % (s + 1)]
-        w, h = T["wt%d" % _slot(s)], T["h%d" % _slot(s)]
-        if s == 0:
-            for m in range(NB):
-                te.wait_ge(sem["lx%d" % m], 16)
-        elif SITE[s - 1] == r:
-            te.wait_ge(sem["c_%d" % (s - 1)], 1)
-        else:
-            te.wait_ge(sem["aa%d" % s], EA)
-        for i in range(2):
-            if s == r:
-                te.wait_ge(sem["lw%d" % i], 16)
-            else:
-                te.wait_ge(sem["ww%d_%d" % (s, i)], EW)
-            for f in range(FT):
-                if i == 0:
-                    te.matmul(out=T["ph%d" % f][:, 0:COLS], lhsT=w[:, f * P:(f + 1) * P], rhs=a_in[:],
-                              start=True, stop=True).then_inc(sem["m1_%d_%d" % (s, f)], 1)
-                else:
-                    te.wait_ge(sem["r_%d_%d" % (s, f)], 1)
-                    te.matmul(out=T.po[:, 0:COLS], lhsT=w[:, WC + f * P:WC + (f + 1) * P],
-                              rhs=h[:, f * COLS:(f + 1) * COLS],
-                              start=(f == 0), stop=(f == FT - 1)).then_inc(sem["m2_%d" % s], 1)
-        for f in range(FT):
-            ve.wait_ge(sem["m1_%d_%d" % (s, f)], 1)
-            ve.tensor_tensor(out=h[:, f * COLS:(f + 1) * COLS], in0=T["ph%d" % f][:, 0:COLS], in1=T.zero[:],
-                             op=AluOpType.max).then_inc(sem["r_%d_%d" % (s, f)], 1)
-        ve.wait_ge(sem["m2_%d" % s], FT)
-        ve.tensor_copy(out=a_out[:], in_=T.po[:, 0:COLS]).then_inc(sem["c_%d" % s], 1)
-
-        if s == N - 1:
-            g.sync.wait_ge(sem["c_%d" % s], 1)
-            g.scalar.wait_ge(sem["c_%d" % s], 1)
-            for m in range(NB):
-                q = g.sync if m % 2 == 0 else g.scalar
-                q.dma_start(T.y[m], a_out[:, m * TK:(m + 1) * TK]).then_inc(sem["st%d" % m], 16)
-            for m in range(NB):
-                g.wait_ge(sem["st%d" % m], 16)
-        elif SITE[s + 1] != r:
-            dst = T.cores[SITE[s + 1]]
-            rid, pid = topo.addr(dst, core)
-            g.wait_ge(sem["c_%d" % s], 1)
-            g.remote_dma(out_ap=a_out[:], in_ap=a_out[:], remote_sem=sem["aa%d" % (s + 1)], local_sem=sem.snt,
-                         pid=pid, routing_id=rid, dma_engine_mask=_engines(topo.mask(core, dst), EA))
-            sent += EA
-
-    if sent:
-        g.wait_ge(sem.snt, sent)
+    if sent[0]:
+        g.wait_ge(sem.snt, sent[0])

@@ -3,6 +3,8 @@ from concourse.mybir import AluOpType
 N, NB, TK, FT = 4, 4, 32, 4
 P = 128
 COLS = NB * TK
+HC = COLS // 2
+PO = 256
 WC = FT * P
 OFF = FT - 1
 KEEP = OFF * P
@@ -10,8 +12,7 @@ EW = 8
 EA = 8
 
 SCRATCH = {
-    "zero": ("sbuf", [P, COLS], "float32"),
-    "po": ("psum", [P, 512], "float32"),
+    "zero": ("sbuf", [P, HC], "float32"),
     "wt0": ("sbuf", [P, 2 * WC], "bfloat16"),
     "wt1": ("sbuf", [P, 2 * WC], "bfloat16"),
     "tw": ("sbuf", [P, 2 * P], "bfloat16"),
@@ -21,15 +22,15 @@ for _k in range(3):
     SCRATCH["h%d" % _k] = ("sbuf", [P, FT * COLS], "bfloat16")
 for _s in range(N + 1):
     SCRATCH["a%d" % _s] = ("sbuf", [P, COLS], "bfloat16")
-for _f in range(FT):
-    SCRATCH["ph%d" % _f] = ("psum", [P, 512], "float32")
+for _q in range(2 * FT):
+    SCRATCH["ph%d" % _q] = ("psum", [P, 512], "float32")
 
 TAGS = ["s0", "s1", "s2", "s3", "t"]
-SEMAPHORES = ["z", "snt", "lw0", "lw1", "lt0", "lt1", "ww0", "ww1", "tarr", "aa1", "aa2", "pbarr"]
-SEMAPHORES += ["lx%d" % m for m in range(NB)] + ["st%d" % m for m in range(NB)]
-SEMAPHORES += ["m1_%s_%d" % (t, f) for t in TAGS for f in range(FT)]
-SEMAPHORES += ["r_%s_%d" % (t, f) for t in TAGS for f in range(FT)]
-SEMAPHORES += ["m2_%s" % t for t in TAGS] + ["c_%s" % t for t in TAGS]
+SEMAPHORES = ["z", "snt", "la", "lb", "lw", "lw0", "lw1", "lt", "ww0", "ww1", "tarr", "aa1", "aa2", "pbarr", "st"]
+SEMAPHORES += ["m1_%s_%d" % (t, q) for t in TAGS for q in range(2 * FT)]
+SEMAPHORES += ["r_%s_%d" % (t, q) for t in TAGS for q in range(2 * FT)]
+SEMAPHORES += ["m2_%s_%d" % (t, k) for t in TAGS for k in range(2)]
+SEMAPHORES += ["c_%s_%d" % (t, k) for t in TAGS for k in range(2)]
 
 
 def _engines(mask, n):
@@ -43,24 +44,35 @@ def _engines(mask, n):
 
 def _map(g, T, tag, tiles, w1, w2, parts, w2waits, h, out):
     te, ve, sem = g.tensor, g.vector, T.sem
-    for pi, (rhs, waits) in enumerate(parts):
+    tiles = list(tiles)
+    for pi, (rhs, waits, hwaits) in enumerate(parts):
         for name, val in waits:
             te.wait_ge(sem[name], val)
-        for f in tiles:
-            te.matmul(out=T["ph%d" % f][:, 0:COLS], lhsT=w1(f), rhs=rhs[:],
-                      start=(pi == 0), stop=(pi == len(parts) - 1)).then_inc(sem["m1_%s_%d" % (tag, f)], 1)
+        for k in range(2):
+            for name, val in hwaits[k]:
+                te.wait_ge(sem[name], val)
+            for f in tiles:
+                q = FT * k + f
+                te.matmul(out=T["ph%d" % q][:, 0:HC], lhsT=w1(f), rhs=rhs[:, k * HC:(k + 1) * HC],
+                          start=(pi == 0), stop=(pi == len(parts) - 1)).then_inc(sem["m1_%s_%d" % (tag, q)], 1)
     for name, val in w2waits:
         te.wait_ge(sem[name], val)
-    for j, f in enumerate(tiles):
-        te.wait_ge(sem["r_%s_%d" % (tag, f)], 1)
-        te.matmul(out=T.po[:, 0:COLS], lhsT=w2(f), rhs=h[:, f * COLS:(f + 1) * COLS],
-                  start=(j == 0), stop=(j == len(tiles) - 1)).then_inc(sem["m2_%s" % tag], 1)
-    for f in tiles:
-        ve.wait_ge(sem["m1_%s_%d" % (tag, f)], len(parts))
-        ve.tensor_tensor(out=h[:, f * COLS:(f + 1) * COLS], in0=T["ph%d" % f][:, 0:COLS], in1=T.zero[:],
-                         op=AluOpType.max).then_inc(sem["r_%s_%d" % (tag, f)], 1)
-    ve.wait_ge(sem["m2_%s" % tag], len(tiles))
-    ve.tensor_copy(out=out[:], in_=T.po[:, 0:COLS]).then_inc(sem["c_%s" % tag], 1)
+    for k in range(2):
+        for j, f in enumerate(tiles):
+            te.wait_ge(sem["r_%s_%d" % (tag, FT * k + f)], 1)
+            te.matmul(out=T["ph%d" % (FT * k)][:, PO:PO + HC], lhsT=w2(f),
+                      rhs=h[:, f * COLS + k * HC:f * COLS + (k + 1) * HC],
+                      start=(j == 0), stop=(j == len(tiles) - 1)).then_inc(sem["m2_%s_%d" % (tag, k)], 1)
+    for k in range(2):
+        for f in tiles:
+            q = FT * k + f
+            ve.wait_ge(sem["m1_%s_%d" % (tag, q)], len(parts))
+            ve.tensor_tensor(out=h[:, f * COLS + k * HC:f * COLS + (k + 1) * HC], in0=T["ph%d" % q][:, 0:HC],
+                             in1=T.zero[:], op=AluOpType.max).then_inc(sem["r_%s_%d" % (tag, q)], 1)
+    for k in range(2):
+        ve.wait_ge(sem["m2_%s_%d" % (tag, k)], len(tiles))
+        ve.tensor_copy(out=out[:, k * HC:(k + 1) * HC], in_=T["ph%d" % (FT * k)][:, PO:PO + HC]).then_inc(
+            sem["c_%s_%d" % (tag, k)], 1)
 
 
 def rank_program(g, core, T, topo):
@@ -70,6 +82,7 @@ def rank_program(g, core, T, topo):
     sem = T.sem
     last = N - 1
     sent = [0]
+    none = ([], [])
 
     def write(dst_rank, dst_ap, src_ap, arrive, n):
         dst = T.cores[dst_rank]
@@ -81,37 +94,46 @@ def rank_program(g, core, T, topo):
     def tiles_of(w):
         return (lambda f: w[:, f * P:(f + 1) * P]), (lambda f: w[:, WC + f * P:WC + (f + 1) * P])
 
+    def halves_of(tag):
+        return ([("c_%s_0" % tag, 1)], [("c_%s_1" % tag, 1)])
+
+    def whole(tag):
+        for k in range(2):
+            g.wait_ge(sem["c_%s_%d" % (tag, k)], 1)
+
     if r != 2:
         g.vector.memset(T.zero[:], 0.0).then_inc(sem.z, 1)
         g.vector.wait_ge(sem.z, 1)
 
     if r == 0:
-        g.sync.dma_start(T.wt0[:, 0:WC], T.w1[:, :]).then_inc(sem.lw0, 16)
-        for m in range(NB):
-            q = g.sync if m < NB // 2 else g.scalar
-            q.dma_start(T.a0[:, m * TK:(m + 1) * TK], T.x[m]).then_inc(sem["lx%d" % m], 16)
+        def load_x(q, m, s):
+            q.dma_start(T.a0[:, m * TK:(m + 1) * TK], T.x[m]).then_inc(sem[s], 16)
+
+        g.sync.dma_start(T.wt0[:, 0:WC], T.w1[:, :]).then_inc(sem.la, 16)
+        load_x(g.scalar, 0, "la")
+        load_x(g.sync, 1, "la")
+        load_x(g.scalar, 2, "lb")
+        load_x(g.sync, 3, "lb")
         g.scalar.dma_start(T.wt0[:, WC:2 * WC], T.w2[:, :]).then_inc(sem.lw1, 16)
         w1, w2 = tiles_of(T.wt0)
-        _map(g, T, "s0", range(FT), w1, w2, [(T.a0, [("lx%d" % m, 16) for m in range(NB)] + [("lw0", 16)])],
-             [("lw1", 16)], T.h0, T.a1)
-        g.wait_ge(sem.c_s0, 1)
+        _map(g, T, "s0", range(FT), w1, w2, [(T.a0, [], ([("la", 48)], [("lb", 32)]))], [("lw1", 16)], T.h0, T.a1)
+        whole("s0")
         write(1, T.a1[:], T.a1[:], "aa1", EA)
         _map(g, T, "t", [OFF], lambda f: T.tw[:, 0:P], lambda f: T.tw[:, P:2 * P],
-             [(T.a1, [("c_s0", 1), ("tarr", EW)])], [], T.h2, T.pb)
-        g.wait_ge(sem.c_t, 1)
+             [(T.a1, [("c_s0_0", 1), ("c_s0_1", 1), ("tarr", EW)], none)], [], T.h2, T.pb)
+        whole("t")
         write(last, T.pb[:], T.pb[:], "pbarr", EA)
 
     if r == 1:
-        g.sync.dma_start(T.tw[:, 0:P], T.w1[:, KEEP:WC]).then_inc(sem.lt0, 16)
-        g.scalar.dma_start(T.tw[:, P:2 * P], T.w2[:, KEEP:WC]).then_inc(sem.lt1, 16)
-        g.sync.dma_start(T.wt0[:, 0:KEEP], T.w1[:, 0:KEEP]).then_inc(sem.lw0, 16)
-        g.scalar.dma_start(T.wt0[:, WC:WC + KEEP], T.w2[:, 0:KEEP]).then_inc(sem.lw1, 16)
-        g.wait_ge(sem.lt0, 16)
-        g.wait_ge(sem.lt1, 16)
+        g.sync.dma_start(T.tw[:, 0:P], T.w1[:, KEEP:WC]).then_inc(sem.lt, 16)
+        g.scalar.dma_start(T.tw[:, P:2 * P], T.w2[:, KEEP:WC]).then_inc(sem.lt, 16)
+        g.sync.dma_start(T.wt0[:, 0:KEEP], T.w1[:, 0:KEEP]).then_inc(sem.lw, 16)
+        g.scalar.dma_start(T.wt0[:, WC:WC + KEEP], T.w2[:, 0:KEEP]).then_inc(sem.lw, 16)
+        g.wait_ge(sem.lt, 32)
         write(0, T.tw[:], T.tw[:], "tarr", EW)
         w1, w2 = tiles_of(T.wt0)
-        _map(g, T, "s1", range(OFF), w1, w2, [(T.a1, [("aa1", EA), ("lw0", 16)])], [("lw1", 16)], T.h0, T.a2)
-        g.wait_ge(sem.c_s1, 1)
+        _map(g, T, "s1", range(OFF), w1, w2, [(T.a1, [("lw", 32), ("aa1", EA)], none)], [], T.h0, T.a2)
+        whole("s1")
         write(last, T.a2[:], T.a2[:], "aa2", EA)
 
     if r == 2:
@@ -122,20 +144,20 @@ def rank_program(g, core, T, topo):
             write(last, T.wt0[:, i * WC:(i + 1) * WC], T.wt0[:, i * WC:(i + 1) * WC], "ww%d" % i, EW)
 
     if r == last:
-        g.sync.dma_start(T.wt1[:, 0:WC], T.w1[:, :]).then_inc(sem.lw0, 16)
-        g.scalar.dma_start(T.wt1[:, WC:2 * WC], T.w2[:, :]).then_inc(sem.lw1, 16)
+        g.sync.dma_start(T.wt1[:, 0:WC], T.w1[:, :]).then_inc(sem.lw, 16)
+        g.scalar.dma_start(T.wt1[:, WC:2 * WC], T.w2[:, :]).then_inc(sem.lw, 16)
         w1, w2 = tiles_of(T.wt0)
-        _map(g, T, "s2", range(FT), w1, w2, [(T.pb, [("pbarr", EA), ("ww0", EW)]), (T.a2, [("aa2", EA)])],
+        _map(g, T, "s2", range(FT), w1, w2,
+             [(T.pb, [("lw", 32), ("pbarr", EA), ("ww0", EW)], none), (T.a2, [("aa2", EA)], none)],
              [("ww1", EW)], T.h0, T.a3)
         w1, w2 = tiles_of(T.wt1)
-        _map(g, T, "s3", range(FT), w1, w2, [(T.a3, [("c_s2", 1), ("lw0", 16)])], [("lw1", 16)], T.h1, T.a4)
-        g.sync.wait_ge(sem.c_s3, 1)
-        g.scalar.wait_ge(sem.c_s3, 1)
-        for m in range(NB):
-            q = g.sync if m % 2 == 0 else g.scalar
-            q.dma_start(T.y[m], T.a4[:, m * TK:(m + 1) * TK]).then_inc(sem["st%d" % m], 16)
-        for m in range(NB):
-            g.wait_ge(sem["st%d" % m], 16)
+        _map(g, T, "s3", range(FT), w1, w2, [(T.a3, [], halves_of("s2"))], [], T.h1, T.a4)
+        for k in range(2):
+            for i, q in enumerate((g.sync, g.scalar)):
+                m = 2 * k + i
+                q.wait_ge(sem["c_s3_%d" % k], 1)
+                q.dma_start(T.y[m], T.a4[:, m * TK:(m + 1) * TK]).then_inc(sem.st, 16)
+        g.wait_ge(sem.st, 16 * NB)
 
     if sent[0]:
         g.wait_ge(sem.snt, sent[0])

from concourse.mybir import AluOpType

N, NB, TK, FT = 4, 4, 32, 4
P = 128
COLS = NB * TK
HC = COLS // 2
PO = 256
WC = FT * P
OFF = FT - 1
KEEP = OFF * P
EW = 8
EA = 8

SCRATCH = {
    "zero": ("sbuf", [P, HC], "float32"),
    "wt0": ("sbuf", [P, 2 * WC], "bfloat16"),
    "wt1": ("sbuf", [P, 2 * WC], "bfloat16"),
    "tw": ("sbuf", [P, 2 * P], "bfloat16"),
    "pb": ("sbuf", [P, COLS], "bfloat16"),
}
for _k in range(3):
    SCRATCH["h%d" % _k] = ("sbuf", [P, FT * COLS], "bfloat16")
for _s in range(N + 1):
    SCRATCH["a%d" % _s] = ("sbuf", [P, COLS], "bfloat16")
for _q in range(2 * FT):
    SCRATCH["ph%d" % _q] = ("psum", [P, 512], "float32")

TAGS = ["s0", "s1", "s2", "s3", "t"]
SEMAPHORES = ["z", "snt", "la", "lb", "lw", "lw0", "lw1", "lt", "ww0", "ww1", "tarr", "aa1", "aa2", "pbarr", "st"]
SEMAPHORES += ["m1_%s_%d" % (t, q) for t in TAGS for q in range(2 * FT)]
SEMAPHORES += ["r_%s_%d" % (t, q) for t in TAGS for q in range(2 * FT)]
SEMAPHORES += ["m2_%s_%d" % (t, k) for t in TAGS for k in range(2)]
SEMAPHORES += ["c_%s_%d" % (t, k) for t in TAGS for k in range(2)]


def _engines(mask, n):
    bits = [b for b in range(16) if (mask >> b) & 1]
    step = max(1, len(bits) // n)
    out = 0
    for b in bits[::step][:n]:
        out |= 1 << b
    return out


def _map(g, T, tag, tiles, w1, w2, parts, w2waits, h, out):
    te, ve, sem = g.tensor, g.vector, T.sem
    tiles = list(tiles)
    for pi, (rhs, waits, hwaits) in enumerate(parts):
        for name, val in waits:
            te.wait_ge(sem[name], val)
        for k in range(2):
            for name, val in hwaits[k]:
                te.wait_ge(sem[name], val)
            for f in tiles:
                q = FT * k + f
                te.matmul(out=T["ph%d" % q][:, 0:HC], lhsT=w1(f), rhs=rhs[:, k * HC:(k + 1) * HC],
                          start=(pi == 0), stop=(pi == len(parts) - 1)).then_inc(sem["m1_%s_%d" % (tag, q)], 1)
    for name, val in w2waits:
        te.wait_ge(sem[name], val)
    for k in range(2):
        for j, f in enumerate(tiles):
            te.wait_ge(sem["r_%s_%d" % (tag, FT * k + f)], 1)
            te.matmul(out=T["ph%d" % (FT * k)][:, PO:PO + HC], lhsT=w2(f),
                      rhs=h[:, f * COLS + k * HC:f * COLS + (k + 1) * HC],
                      start=(j == 0), stop=(j == len(tiles) - 1)).then_inc(sem["m2_%s_%d" % (tag, k)], 1)
    for k in range(2):
        for f in tiles:
            q = FT * k + f
            ve.wait_ge(sem["m1_%s_%d" % (tag, q)], len(parts))
            ve.tensor_tensor(out=h[:, f * COLS + k * HC:f * COLS + (k + 1) * HC], in0=T["ph%d" % q][:, 0:HC],
                             in1=T.zero[:], op=AluOpType.max).then_inc(sem["r_%s_%d" % (tag, q)], 1)
    for k in range(2):
        ve.wait_ge(sem["m2_%s_%d" % (tag, k)], len(tiles))
        ve.tensor_copy(out=out[:, k * HC:(k + 1) * HC], in_=T["ph%d" % (FT * k)][:, PO:PO + HC]).then_inc(
            sem["c_%s_%d" % (tag, k)], 1)


def rank_program(g, core, T, topo):
    r = T.rank_of(core)
    if r is None:
        return
    sem = T.sem
    last = N - 1
    sent = [0]
    none = ([], [])

    def write(dst_rank, dst_ap, src_ap, arrive, n):
        dst = T.cores[dst_rank]
        rid, pid = topo.addr(dst, core)
        g.remote_dma(out_ap=dst_ap, in_ap=src_ap, remote_sem=sem[arrive], local_sem=sem.snt,
                     pid=pid, routing_id=rid, dma_engine_mask=_engines(topo.mask(core, dst), n))
        sent[0] += n

    def tiles_of(w):
        return (lambda f: w[:, f * P:(f + 1) * P]), (lambda f: w[:, WC + f * P:WC + (f + 1) * P])

    def halves_of(tag):
        return ([("c_%s_0" % tag, 1)], [("c_%s_1" % tag, 1)])

    def whole(tag):
        for k in range(2):
            g.wait_ge(sem["c_%s_%d" % (tag, k)], 1)

    if r != 2:
        g.vector.memset(T.zero[:], 0.0).then_inc(sem.z, 1)
        g.vector.wait_ge(sem.z, 1)

    if r == 0:
        def load_x(q, m, s):
            q.dma_start(T.a0[:, m * TK:(m + 1) * TK], T.x[m]).then_inc(sem[s], 16)

        g.sync.dma_start(T.wt0[:, 0:WC], T.w1[:, :]).then_inc(sem.la, 16)
        load_x(g.scalar, 0, "la")
        load_x(g.sync, 1, "la")
        load_x(g.scalar, 2, "lb")
        load_x(g.sync, 3, "lb")
        g.scalar.dma_start(T.wt0[:, WC:2 * WC], T.w2[:, :]).then_inc(sem.lw1, 16)
        w1, w2 = tiles_of(T.wt0)
        _map(g, T, "s0", range(FT), w1, w2, [(T.a0, [], ([("la", 48)], [("lb", 32)]))], [("lw1", 16)], T.h0, T.a1)
        whole("s0")
        write(1, T.a1[:], T.a1[:], "aa1", EA)
        _map(g, T, "t", [OFF], lambda f: T.tw[:, 0:P], lambda f: T.tw[:, P:2 * P],
             [(T.a1, [("c_s0_0", 1), ("c_s0_1", 1), ("tarr", EW)], none)], [], T.h2, T.pb)
        whole("t")
        write(last, T.pb[:], T.pb[:], "pbarr", EA)

    if r == 1:
        g.sync.dma_start(T.tw[:, 0:P], T.w1[:, KEEP:WC]).then_inc(sem.lt, 16)
        g.scalar.dma_start(T.tw[:, P:2 * P], T.w2[:, KEEP:WC]).then_inc(sem.lt, 16)
        g.sync.dma_start(T.wt0[:, 0:KEEP], T.w1[:, 0:KEEP]).then_inc(sem.lw, 16)
        g.scalar.dma_start(T.wt0[:, WC:WC + KEEP], T.w2[:, 0:KEEP]).then_inc(sem.lw, 16)
        g.wait_ge(sem.lt, 32)
        write(0, T.tw[:], T.tw[:], "tarr", EW)
        w1, w2 = tiles_of(T.wt0)
        _map(g, T, "s1", range(OFF), w1, w2, [(T.a1, [("lw", 32), ("aa1", EA)], none)], [], T.h0, T.a2)
        whole("s1")
        write(last, T.a2[:], T.a2[:], "aa2", EA)

    if r == 2:
        g.sync.dma_start(T.wt0[:, 0:WC], T.w1[:, :]).then_inc(sem.lw0, 16)
        g.scalar.dma_start(T.wt0[:, WC:2 * WC], T.w2[:, :]).then_inc(sem.lw1, 16)
        for i in range(2):
            g.wait_ge(sem["lw%d" % i], 16)
            write(last, T.wt0[:, i * WC:(i + 1) * WC], T.wt0[:, i * WC:(i + 1) * WC], "ww%d" % i, EW)

    if r == last:
        g.sync.dma_start(T.wt1[:, 0:WC], T.w1[:, :]).then_inc(sem.lw, 16)
        g.scalar.dma_start(T.wt1[:, WC:2 * WC], T.w2[:, :]).then_inc(sem.lw, 16)
        w1, w2 = tiles_of(T.wt0)
        _map(g, T, "s2", range(FT), w1, w2,
             [(T.pb, [("lw", 32), ("pbarr", EA), ("ww0", EW)], none), (T.a2, [("aa2", EA)], none)],
             [("ww1", EW)], T.h0, T.a3)
        w1, w2 = tiles_of(T.wt1)
        _map(g, T, "s3", range(FT), w1, w2, [(T.a3, [], halves_of("s2"))], [], T.h1, T.a4)
        for k in range(2):
            for i, q in enumerate((g.sync, g.scalar)):
                m = 2 * k + i
                q.wait_ge(sem["c_s3_%d" % k], 1)
                q.dma_start(T.y[m], T.a4[:, m * TK:(m + 1) * TK]).then_inc(sem.st, 16)
        g.wait_ge(sem.st, 16 * NB)

    if sent[0]:
        g.wait_ge(sem.snt, sent[0])
